import numpy as np
CORES = [97,101,225,229,353,357,481,485]
N = 8
HOST = [c // 128 for c in CORES]
HS = sorted(set(HOST)); H = len(HS)
R, T = 4096, 1024
def entries(a): return a.T.reshape(-1)
def pack(v, P): return np.ascontiguousarray(np.asarray(v, np.int32).reshape(-1, P).T)
def lists(rng, how):
    A = np.array(HOST); L = [rng.permutation(N * R)[:T] for h in HS]
    if how == "away": L = [R * int(rng.choice(np.flatnonzero(A != h))) + rng.permutation(R)[:T] for h in HS]
    if how == "edge": E = R * np.arange(N); E = np.concatenate([E, E + R - 1]); F = np.setdiff1d(np.arange(N * R), E); L = [rng.permutation(np.concatenate([E, rng.permutation(F)[:T - 2 * N]])) for h in HS]
    if how == "home": O = np.repeat(A, R); L = [rng.permutation(np.flatnonzero(O == h))[:T] for h in HS]
    if how == "hotrank": z = R * int(rng.integers(N)); L = [z + rng.permutation(R)[:T] for h in HS]
    if how == "meet": L = [rng.permutation(L[0]) for h in HS]
    return {"idx": np.stack([pack(L[HS.index(HOST[r])], 16) for r in range(N)])}
def setup_inputs(rng):
    return dict({"g": rng.standard_normal((N, 128, T), dtype=np.float32)}, **lists(rng, "uniform"))
def setup_inputs_away(rng):
    d = setup_inputs(rng); d.update(lists(rng, "away"))
    for k in ("g",): d[k] = (d[k].astype(np.float32) * 1024.0).astype(d[k].dtype)
    return d
def setup_inputs_edge(rng):
    d = setup_inputs(rng); d.update(lists(rng, "edge"))
    for k in ("g",): d[k] = (d[k].astype(np.float32) * (1 / 1024.0)).astype(d[k].dtype)
    return d
def setup_inputs_home(rng):
    d = setup_inputs(rng); d.update(lists(rng, "home"))
    return d
def setup_inputs_hotrank(rng):
    d = setup_inputs(rng); d.update(lists(rng, "hotrank"))
    return d
def setup_inputs_meet(rng):
    d = setup_inputs(rng); d.update(lists(rng, "meet"))
    return d
def check_inputs(x):
    bad = []
    if x["idx"].min() < 0 or x["idx"].max() >= N * R: bad.append("idx out of range")
    if any(len(np.unique(a)) != a.size for a in x["idx"]): bad.append("a number stands twice in a list")
    if any(HOST[p] == HOST[s] and not np.array_equal(x["idx"][p], x["idx"][s]) for p in range(N) for s in range(p)): bad.append("two ranks of one host hold different lists")
    return bad
def reference(g, idx):
    S = np.zeros((128, N * R))
    for q in range(N):
        I = entries(idx[q]); S[:, I] += g[q].astype(np.float64)
    return {"y": np.stack([S[:, R * r:R * r + R] for r in range(N)]).astype(np.float32)}

@@ -1,0 +1,410 @@
+from concourse.bass import DstId, RemoteDMATransfer
+from concourse.mybir import AluOpType as A, ActivationFunctionType as AF
+
+B = 1024
+Z = 4
+VW = Z + 4 * B
+R = 4096
+PARTS = ((0, 0, 512), (1, 512, 1024), (0, 1024, 2560), (1, 2560, 4096))
+
+SCRATCH = {
+    "V": ("sbuf", [128, VW], "float32"),
+    "Y": ("sbuf", [128, R], "float32"),
+    "H": ("sbuf", [128, 512], "float32"),
+    "SEND": ("sbuf", [128, 512], "float32"),
+    "GO": ("sbuf", [128, 512], "float32"),
+    "X": ("sbuf", [128, 512], "float32"),
+    "IX": ("sbuf", [128, 8], "int32"),
+    "K": ("sbuf", [128, 32], "int32"),
+    "PL": ("sbuf", [128, 128], "float32"),
+    "HL": ("sbuf", [128, 16], "float32"),
+    "PI": ("sbuf", [128, 4], "int32"), "MI": ("sbuf", [128, 128], "int32"),
+    "CI": ("sbuf", [128, 8], "int32"), "CF": ("sbuf", [128, 8], "float32"), "CG": ("sbuf", [128, 4], "float32"),
+    "J0": ("sbuf", [128, 8], "float32"), "J": ("sbuf", [128, 8], "float32"),
+    "IM": ("sbuf", [128, 128], "float16"), "IN": ("sbuf", [128, 32], "float16"),
+    "R15": ("sbuf", [128, 128], "int32"), "R16": ("sbuf", [128, 128], "int32"),
+    "R2": ("sbuf", [128, 128], "int32"), "R1": ("sbuf", [128, 128], "int32"), "R8": ("sbuf", [128, 16], "int32"),
+    "ID": ("sbuf", [128, 128], "float32"), "B1": ("sbuf", [128, 128], "float32"), "B2": ("sbuf", [128, 128], "float32"),
+    "B3": ("sbuf", [128, 64], "float32"), "BD": ("sbuf", [128, 128], "bfloat16"), "MS": ("sbuf", [128, 128], "bfloat16"),
+    "TC": ("sbuf", [128, 8], "uint16"), "RO": ("sbuf", [128, 16], "uint16"),
+    "LT": ("sbuf", [128, 4 * 1024], "float16"), "RH": ("sbuf", [128, 4 * 256], "float16"),
+    "L": ("sbuf", [128, 128], "float32"), "U": ("sbuf", [128, 128], "float32"), "W": ("sbuf", [128, 128], "float32"),
+    "TR": ("sbuf", [128, 4 * 256], "float32"), "TAB": ("sbuf", [128, 3 * 264], "float32"),
+    "OF": ("sbuf", [128, 32], "float32"), "OU": ("sbuf", [128, 32], "uint16"),
+    "E": ("sbuf", [128, 512], "bfloat16"), "EQ": ("sbuf", [128, 512], "float32"),
+    "GM": ("sbuf", [128, 512], "float32"), "ZM": ("sbuf", [128, 512], "float32"),
+    "PV": ("sbuf", [128, 256], "uint16"), "LST": ("sbuf", [128, 256], "uint16"),
+    "PT0": ("psum", [128, 512], "float32"), "PT1": ("psum", [128, 512], "float32"),
+    "PX0": ("psum", [128, 512], "float32"), "PX1": ("psum", [128, 512], "float32"),
+    "PC": ("psum", [128, 512], "float32"), "PM": ("psum", [128, 512], "float32"), "PN": ("psum", [128, 512], "float32"),
+}
+REMOTE = ["ls", "hl", "h0", "h1", "xs", "ps", "l1", "l2", "l3", "b1", "b2", "d0", "d1"]
+SEMAPHORES = REMOTE + ["ix", "gp", "go", "ys"] + ["s%d" % i for i in range(100)]
+
+
+def bits(mask):
+    return [i for i in range(16) if mask >> i & 1]
+
+
+def engines(l):
+    return sum(1 << i for i in l)
+
+
+def same_chip(topo, a, b):
+    return topo.host(a) == topo.host(b) and topo.chip(a) == topo.chip(b)
+
+
+def peers(topo, T, c):
+    p = [d for d in T.cores if d != c and same_chip(topo, c, d)][0]
+    o = [d for d in T.cores if topo.host(d) != topo.host(c) and topo.die(d) == topo.die(c) and topo.may_write(c, d)]
+    k = [d for d in o if topo.rack(topo.host(d)) == topo.rack(topo.host(c))][0]
+    q = [d for d in o if topo.rack(topo.host(d)) != topo.rack(topo.host(c))][0]
+    return p, k, q
+
+
+def helpers(topo, c):
+    m = [d for d in range(c - 8, c + 9) if d != c and d >= 0 and same_chip(topo, c, d) and topo.die(c) == topo.die(d)]
+    return m[-1], m[-2]
+
+
+def chunk(b, u, s):
+    k = Z + B * b + 512 * u + 256 * s
+    return slice(k, k + 256)
+
+
+def tr(topo, core, src, dst, dests, eng, sem):
+    ids = []
+    for d in dests:
+        rid, pid = topo.addr(d, core)
+        ids.append(DstId(rid=rid, pnc=pid))
+    return RemoteDMATransfer(dst_ids=ids, dma_engine_mask=engines(eng), remote_sem=sem, srcs=[src],
+                             dsts=[dst] * len(ids), alu_op=0)
+
+
+def rank_program(g, core, T, topo):
+    mine = sorted(d for d in T.cores if same_chip(topo, d, core))
+    if not mine:
+        return
+    if T.rank_of(core) is not None:
+        return rank_core(g, core, T, topo, mine.index(core))
+    for s in range(2):
+        hs = helpers(topo, mine[s])
+        if core in hs:
+            return helper_core(g, core, T, topo, s, mine, hs.index(core))
+
+
+def helper_core(g, core, T, topo, s, mine, way):
+    S = T.sem
+    _, k, q = peers(topo, T, mine[s])
+    far = q if way == 0 else k
+    far = sorted(d for d in T.cores if same_chip(topo, d, far))
+    off = bits(topo.mask(core, far[0]))
+    on = [e for e in bits(topo.mask(core, mine[0])) if e not in off]
+    n = [0]
+    lst = T.HL[:, 0:16]
+    def pl(b): return T.PL[:, 32 * b + 16 * s:32 * b + 16 * s + 16]
+    g.wait_ge(S.hl, len(off) // 2)
+    g.remote_dma_fused([tr(topo, core, lst, pl(1 + way), mine, on, S["l%d" % (1 + way)]),
+                        tr(topo, core, lst, pl(3), [far[s ^ way]], off, S.l3)], local_sem=S.ls)
+    n[0] += len(on) + len(off)
+    for u in ((0, 1) if way == 0 else (1, 0)):
+        src = T.H[:, 256 * u:256 * u + 256]
+        g.wait_ge(S["h%d" % u], len(off) // 2)
+        t = [tr(topo, core, src, T.V[:, chunk(1 + way, u, s)], mine, on, S["b%d" % (1 + way)])]
+        n[0] += len(on)
+        if u == way:
+            t = [tr(topo, core, src, T.V[:, chunk(3, u, s)], far, off, S["d%d" % u])] + t
+            n[0] += len(off)
+        g.remote_dma_fused(t, local_sem=S.ls)
+    g.wait_ge(S.ls, n[0])
+
+
+def rank_core(g, core, T, topo, s):
+    S, v, te, sc = T.sem, g.vector, g.tensor, g.scalar
+    r = T.rank_of(core)
+    partner, rackp, cablep = peers(topo, T, core)
+    hr, hc = helpers(topo, rackp)[0], helpers(topo, cablep)[1]
+    off = bits(topo.mask(core, hr))
+    on = [e for e in bits(topo.mask(core, partner)) if e not in off]
+    used = [0]
+
+    def grp():
+        used[0] += 1
+        return [S["s%d" % (used[0] - 1)], 0]
+
+    def inc(G, inst):
+        inst.then_inc(G[0], 1)
+        G[1] += 1
+
+    def wait(queue, *Gs):
+        for G in Gs:
+            queue.wait_ge(G[0], G[1])
+
+    sc.dma_start(T.IX[:], T.idx[:]).then_inc(S.ix, 16)
+    for u in range(2):
+        k = 512 * u + 256 * (1 - s)
+        g.sync.dma_start(T.SEND[:, 256 * u:256 * u + 256], T.g[:, k:k + 256]).then_inc(S.gp, 16)
+    for u in range(2):
+        k = 512 * u + 256 * s
+        g.sync.dma_start(T.GO[:, 256 * u:256 * u + 256], T.g[:, k:k + 256]).then_inc(S.go, 16)
+
+    gi = grp()
+    inc(gi, g.iota(T.PI[:, 0:1], [[0, 1]], 0, 1))
+    inc(gi, g.iota(T.MI[:], [[1, 128]], 0, 0))
+    gz = grp()
+    inc(gz, v.memset(T.V[:, 0:Z], 0.0))
+    inc(gz, v.memset(T.TAB[:], 0.0))
+    wait(v, gi)
+    g1 = grp()
+    P = T.PI[:, 0:1]
+    inc(g1, v.tensor_scalar(T.CI[:, 0:1], P, 15, None, A.bitwise_and))
+    inc(g1, v.tensor_scalar(T.CI[:, 1:2], P, 4, None, A.arith_shift_right))
+    inc(g1, v.tensor_scalar(T.CI[:, 2:3], P, 3, 1, A.arith_shift_right, A.bitwise_and))
+    inc(g1, v.tensor_scalar(T.CI[:, 3:4], P, 7, None, A.bitwise_and))
+    inc(g1, v.tensor_scalar(T.CI[:, 4:5], P, 3, None, A.arith_shift_right))
+    inc(g1, v.tensor_scalar(T.CI[:, 5:6], P, 0, None, A.arith_shift_right))
+    inc(g1, v.tensor_scalar(T.IM[:], T.MI[:], float(128 * r), None, A.add))
+    inc(g1, v.tensor_copy(T.IN[:], T.MI[:, 0:32]))
+    wait(v, g1)
+    g2 = grp()
+    inc(g2, v.tensor_copy(T.CF[:, 0:6], T.CI[:, 0:6]))
+    wait(v, g2)
+    c15, c16, c3, c7, cd8, cp = [T.CF[:, i:i + 1] for i in range(6)]
+    g3 = grp()
+    inc(g3, v.tensor_scalar(T.CG[:, 0:1], c7, 128.0, cd8, A.mult, A.add))
+    inc(g3, v.tensor_scalar(T.CG[:, 1:2], c7, 8.0, c16, A.mult, A.add))
+    wait(v, g3)
+    g4 = grp()
+    inc(g4, v.tensor_scalar(T.J0[:], T.MI[:, 0:8], 16.0, T.CG[:, 0:1], A.mult, A.add))
+    wait(v, g4)
+    g5 = grp()
+    inc(g5, v.tensor_scalar(T.J[:], T.J0[:], float(Z), None, A.add))
+
+    gk = grp()
+    v.wait_ge(S.ix, 16)
+    inc(gk, v.tensor_scalar(T.K[:, 0:8], T.IX[:], 5, None, A.arith_shift_right))
+    inc(gk, v.tensor_scalar(T.K[:, 8:16], T.IX[:], 31, None, A.bitwise_and))
+    inc(gk, v.tensor_scalar(T.K[:, 16:24], T.IX[:], 15, None, A.bitwise_and))
+    inc(gk, v.tensor_scalar(T.K[:, 24:32], T.IX[:], 4, None, A.arith_shift_right))
+    wait(v, gk)
+    gl = grp()
+    inc(gl, v.tensor_copy(T.PL[:, 0:32], T.K[:]))
+    wait(v, gl, g5)
+
+    onehot = {}
+
+    def make_onehot(b):
+        G = onehot[b] = grp()
+        for k in range(8):
+            f = 32 * b + k
+            inc(G, v.tensor_scalar(T.LT[:, 1024 * b + 128 * k:1024 * b + 128 * k + 128], T.IM[:], T.PL[:, f:f + 1], None,
+                                   A.is_equal))
+            inc(G, v.tensor_scalar(T.RH[:, 256 * b + 32 * k:256 * b + 32 * k + 32], T.IN[:], T.PL[:, f + 8:f + 9],
+                                   T.J[:, k:k + 1], A.is_equal, A.mult))
+
+    make_onehot(0)
+    gr = grp()
+    inc(gr, v.tensor_scalar(T.R15[:], T.MI[:], 15, None, A.bitwise_and))
+    inc(gr, v.tensor_scalar(T.R16[:], T.MI[:], 4, None, A.arith_shift_right))
+    inc(gr, v.tensor_scalar(T.R2[:], T.MI[:], 15, 1, A.bitwise_and, A.arith_shift_right))
+    inc(gr, v.tensor_scalar(T.R1[:], T.MI[:], 1, None, A.bitwise_and))
+    inc(gr, v.tensor_scalar(T.R8[:], T.MI[:, 0:16], 8, None, A.bitwise_and))
+    gc = grp()
+    inc(gc, v.tensor_scalar(T.ID[:], T.MI[:], cp, None, A.is_equal))
+    wait(v, gr)
+    inc(gc, v.tensor_scalar(T.RO[:], T.R8[:], 2.0, c15, A.mult, A.add))
+    inc(gc, v.tensor_copy(T.TC[:], T.MI[:, 0:8]))
+    inc(gc, v.tensor_scalar(T.MS[:], T.R15[:], c15, None, A.is_equal))
+    inc(gc, v.tensor_scalar(T.BD[:], T.R16[:], c16, None, A.is_equal))
+    inc(gc, v.tensor_scalar(T.B1[:], T.R2[:], c16, None, A.is_equal))
+    inc(gc, v.tensor_scalar(T.B2[:], T.R1[:], c3, None, A.is_equal))
+    inc(gc, v.tensor_scalar(T.B3[:], T.MI[:, 0:64], T.CG[:, 1:2], None, A.is_equal))
+
+    PT, PX = (T.PT0, T.PT1), (T.PX0, T.PX1)
+    gT, gL, gTR, gX, gTab, gE, gC, gEQ, gGM, gM, gZ, gN, gPV, gOF, gOU, gW = ({} for _ in range(16))
+
+    def pe_map(b):
+        G = gT[b] = grp()
+        wait(te, onehot[b])
+        for k in range(8):
+            inc(G, te.matmul(PT[b % 2][:, 0:32], T.LT[:, 1024 * b + 128 * k:1024 * b + 128 * k + 128],
+                             T.RH[:, 256 * b + 32 * k:256 * b + 32 * k + 32], k == 0, k == 7))
+
+    def merge(b):
+        l = T.L[:, 32 * b:32 * b + 32]
+        t = PT[b % 2][:, 0:32]
+        wait(v, gT[b])
+        if b == 0:
+            G = gL[b] = grp()
+            inc(G, v.tensor_copy(l, t))
+            return
+        u, w = T.U[:, 32 * b:32 * b + 32], T.W[:, 32 * b:32 * b + 32]
+        G = grp()
+        inc(G, v.tensor_scalar(u, t, 0.0, float(B * b), A.is_gt, A.mult))
+        wait(v, G)
+        G = gW[b] = grp()
+        inc(G, v.tensor_tensor(w, t, u, A.add))
+        wait(v, G, gL[b - 1])
+        G = gL[b] = grp()
+        inc(G, v.tensor_tensor(l, w, T.L[:, 32 * b - 32:32 * b], A.max))
+
+    def spread(b):
+        wait(sc, gL[b], gc)
+        G = gTR[b] = grp()
+        inc(G, sc.activation(T.TR[:, 256 * b:256 * b + 256], T.L[:, 32 * b:32 * b + 32].indirect(T.RO[:, 0:16]), AF.Copy))
+
+    def pe_spread(b):
+        G = gX[b] = grp()
+        wait(te, gTR[b], gc)
+        for h in range(2):
+            inc(G, te.matmul(PX[b % 2][:, 128 * h:128 * h + 128], T.TR[:, 256 * b + 128 * h:256 * b + 128 * h + 128], T.ID[:],
+                             True, True))
+
+    def table(b):
+        G = gTab[b] = grp()
+        wait(v, gX[b], gz)
+        for h in range(2):
+            o = 264 * b + 1 + h
+            inc(G, v.tensor_copy(T.TAB[:, o:o + 255:2], PX[b % 2][:, 128 * h:128 * h + 128]))
+
+    def entries(b):
+        q = slice(8 * b, 8 * b + 8)
+        G = gOF[b] = grp()
+        inc(G, v.tensor_scalar(T.OF[:, q], T.PL[:, 32 * b + 24:32 * b + 32], float(256 * r - 1), float(256 * r + 256),
+                               A.max, A.min))
+        wait(v, gc)
+        G = gE[b] = grp()
+        inc(G, v.tensor_tensor(T.E[:, 128 * b:128 * b + 128], T.PL[:, 32 * b + 16:32 * b + 24].indirect(T.TC[:, 0:8]), T.MS[:],
+                               A.mult))
+        wait(v, gOF[b])
+        G = gOU[b] = grp()
+        inc(G, v.tensor_scalar(T.OU[:, q], T.OF[:, q], float(1 - 256 * r), None, A.add))
+
+    def pe_entries(b):
+        G = gC[b] = grp()
+        wait(te, gE[b], gc)
+        inc(G, te.matmul(T.PC[:, 0:128], T.BD[:], T.E[:, 128 * b:128 * b + 128], True, True))
+
+    def lookup(b):
+        q = slice(128 * b, 128 * b + 128)
+        wait(v, gC[b])
+        G = gEQ[b] = grp()
+        inc(G, v.tensor_scalar(T.EQ[:, q], T.PC[:, 0:128], c15, None, A.is_equal))
+        table(b - 1)
+        wait(v, gEQ[b], gTab[b - 1], gOU[b])
+        G = gGM[b] = grp()
+        o = 264 * (b - 1)
+        inc(G, v.tensor_tensor(T.GM[:, q], T.TAB[:, o:o + 258].indirect(T.OU[:, 8 * b:8 * b + 8]), T.EQ[:, q], A.mult))
+
+    def pe_pick(b):
+        q = slice(128 * b, 128 * b + 128)
+        wait(te, gGM[b])
+        G = gM[b] = grp()
+        inc(G, te.matmul(T.PM[:, 0:128], T.GM[:, q], T.B1[:], True, True))
+
+    def picked(b):
+        q = slice(128 * b, 128 * b + 128)
+        wait(v, gM[b])
+        G = gZ[b] = grp()
+        inc(G, v.tensor_tensor(T.ZM[:, q], T.PM[:, 0:128], T.B2[:], A.mult))
+
+    def pe_place(b):
+        q = slice(128 * b, 128 * b + 128)
+        wait(te, gZ[b])
+        if b > 1:
+            wait(te, gPV[b - 1])
+        G = gN[b] = grp()
+        inc(G, te.matmul(T.PN[:, 0:64], T.ZM[:, q], T.B3[:], True, True))
+
+    def prev(b):
+        wait(v, gN[b])
+        G = gPV[b] = grp()
+        inc(G, v.tensor_copy(T.PV[:, 64 * b:64 * b + 64], T.PN[:, 0:64]))
+
+    pe_map(0)
+    merge(0)
+    spread(0)
+    pe_spread(0)
+
+    gS = grp()
+    v.wait_ge(S.go, 32)
+    v.wait_ge(S.xs, 16)
+    for u in range(2):
+        q = slice(256 * u, 256 * u + 256)
+        inc(gS, v.tensor_tensor(T.V[:, chunk(0, u, s)], T.GO[:, q], T.X[:, q], A.add))
+
+    for b in (1, 2, 3):
+        v.wait_ge(S["l%d" % b], 2 * (len(off) if b == 3 else len(on)))
+        make_onehot(b)
+        entries(b)
+        pe_map(b)
+        pe_entries(b)
+        if b > 1:
+            prev(b - 1)
+        lookup(b)
+        pe_pick(b)
+        merge(b)
+        spread(b)
+        pe_spread(b)
+        picked(b)
+        pe_place(b)
+    prev(3)
+    wait(v, gX[3])
+    gLast = grp()
+    for h in range(2):
+        inc(gLast, v.tensor_copy(T.LST[:, h:h + 255:2], PX[1][:, 128 * h:128 * h + 128]))
+
+    gA = [gS, gz]
+
+    def add(b, lo, hi):
+        G = grp()
+        k = Z + B * b
+        inc(G, v.tensor_tensor(T.V[:, k + lo:k + hi],
+                               T.V[:, 0:k].indirect(T.PV[:, 64 * b + lo // 16:64 * b + hi // 16]), T.V[:, k + lo:k + hi], A.add))
+        return G
+
+    wait(v, gPV[1], gPV[2], gPV[3], gLast, gS, gz)
+    v.wait_ge(S.ps, 2 * len(on))
+    v.wait_ge(S.b1, 4 * len(on))
+    G = add(1, 0, B)
+    v.wait_ge(S.b2, 4 * len(on))
+    wait(v, G)
+    G = add(2, 0, B)
+    wait(v, G)
+    v.wait_ge(S.d0, 2 * len(off))
+    G0 = add(3, 0, 512)
+    v.wait_ge(S.d1, 2 * len(off))
+    G1 = add(3, 512, B)
+
+    wait(v, G0, G1)
+    wait(sc, G0, G1, gLast)
+    for who, lo, hi in PARTS:
+        G = grp()
+        win = T.V[:].indirect(T.LST[:, lo // 16:hi // 16])
+        if who:
+            inc(G, v.tensor_copy(T.Y[:, lo:hi], win))
+        else:
+            inc(G, sc.activation(T.Y[:, lo:hi], win, AF.Copy))
+        wait(g.sync, G)
+        g.sync.dma_start(T.y[:, lo:hi], T.Y[:, lo:hi]).then_inc(S.ys, 16)
+    g.sync.wait_ge(S.ys, 16 * len(PARTS))
+
+    wait(g, gl)
+    half = T.PL[:, 16 * s:16 * s + 16]
+    even, odd = off[0::2], off[1::2]
+    g.remote_dma_fused([tr(topo, core, half, T.HL[:, 0:16], [hr], even, S.hl),
+                        tr(topo, core, half, T.HL[:, 0:16], [hc], odd, S.hl)], local_sem=S.ls)
+    n = len(off)
+    g.wait_ge(S.gp, 32)
+    g.remote_dma_fused([tr(topo, core, T.SEND[:, 256 * u:256 * u + 256], T.X[:, 256 * u:256 * u + 256], [partner],
+                           (off, on)[u], S.xs) for u in range(2)], local_sem=S.ls)
+    n += len(off) + len(on)
+    wait(g, gS)
+    for i in range(2):
+        a, b = i, 1 - i
+        g.remote_dma_fused([
+            tr(topo, core, T.V[:, chunk(0, a, s)], T.H[:, 256 * a:256 * a + 256], [hr], even, S["h%d" % a]),
+            tr(topo, core, T.V[:, chunk(0, b, s)], T.H[:, 256 * b:256 * b + 256], [hc], odd, S["h%d" % b]),
+            tr(topo, core, T.V[:, chunk(0, a, s)], T.V[:, chunk(0, a, s)], [partner], on, S.ps)], local_sem=S.ls)
+        n += len(off) + len(on)
+    g.wait_ge(S.ls, n)

@@ -5,7 +5,11 @@ B = 1024
 Z = 4
 VW = Z + 4 * B
 R = 4096
-PARTS = ((0, 0, 512), (1, 512, 1024), (0, 1024, 2560), (1, 2560, 4096))
+CUTS = (0, 320, 1024, 2048)
+
+BASE = (0, 16, 48)
+LOHI = (None, 16, 64)
+WIDE = (8, 16, 8)
 
 SCRATCH = {
     "V": ("sbuf", [128, VW], "float32"),
@@ -15,30 +19,33 @@ SCRATCH = {
     "GO": ("sbuf", [128, 512], "float32"),
     "X": ("sbuf", [128, 512], "float32"),
     "IX": ("sbuf", [128, 8], "int32"),
-    "K": ("sbuf", [128, 32], "int32"),
-    "PL": ("sbuf", [128, 128], "float32"),
-    "HL": ("sbuf", [128, 16], "float32"),
-    "PI": ("sbuf", [128, 4], "int32"), "MI": ("sbuf", [128, 128], "int32"),
+    "IR": ("sbuf", [128, 24], "int32"),
+    "HL": ("sbuf", [128, 8], "int32"),
+    "K": ("sbuf", [128, 112], "int32"), "PL": ("sbuf", [128, 112], "float32"),
+    "PI": ("sbuf", [128, 4], "int32"), "MI": ("sbuf", [128, 256], "int32"), "JI": ("sbuf", [128, 8], "int32"),
     "CI": ("sbuf", [128, 8], "int32"), "CF": ("sbuf", [128, 8], "float32"), "CG": ("sbuf", [128, 4], "float32"),
-    "J0": ("sbuf", [128, 8], "float32"), "J": ("sbuf", [128, 8], "float32"),
+    "J": ("sbuf", [128, 8], "float32"),
     "IM": ("sbuf", [128, 128], "float16"), "IN": ("sbuf", [128, 32], "float16"),
-    "R15": ("sbuf", [128, 128], "int32"), "R16": ("sbuf", [128, 128], "int32"),
+    "R15": ("sbuf", [128, 256], "int32"), "R16": ("sbuf", [128, 128], "int32"),
     "R2": ("sbuf", [128, 128], "int32"), "R1": ("sbuf", [128, 128], "int32"), "R8": ("sbuf", [128, 16], "int32"),
     "ID": ("sbuf", [128, 128], "float32"), "B1": ("sbuf", [128, 128], "float32"), "B2": ("sbuf", [128, 128], "float32"),
-    "B3": ("sbuf", [128, 64], "float32"), "BD": ("sbuf", [128, 128], "bfloat16"), "MS": ("sbuf", [128, 128], "bfloat16"),
-    "TC": ("sbuf", [128, 8], "uint16"), "RO": ("sbuf", [128, 16], "uint16"),
-    "LT": ("sbuf", [128, 4 * 1024], "float16"), "RH": ("sbuf", [128, 4 * 256], "float16"),
-    "L": ("sbuf", [128, 128], "float32"), "U": ("sbuf", [128, 128], "float32"), "W": ("sbuf", [128, 128], "float32"),
+    "B3": ("sbuf", [128, 64], "float32"), "BD": ("sbuf", [128, 128], "bfloat16"), "MS": ("sbuf", [128, 256], "bfloat16"),
+    "TC": ("sbuf", [128, 16], "uint16"), "RO": ("sbuf", [128, 16], "uint16"),
+    "LT": ("sbuf", [128, 2 * 1024], "float16"), "RH": ("sbuf", [128, 2 * 256], "float16"),
+    "L": ("sbuf", [128, 128], "float32"), "U": ("sbuf", [128, 32], "float32"), "W": ("sbuf", [128, 32], "float32"),
     "TR": ("sbuf", [128, 4 * 256], "float32"), "TAB": ("sbuf", [128, 3 * 264], "float32"),
     "OF": ("sbuf", [128, 32], "float32"), "OU": ("sbuf", [128, 32], "uint16"),
     "E": ("sbuf", [128, 512], "bfloat16"), "EQ": ("sbuf", [128, 512], "float32"),
     "GM": ("sbuf", [128, 512], "float32"), "ZM": ("sbuf", [128, 512], "float32"),
     "PV": ("sbuf", [128, 256], "uint16"), "LST": ("sbuf", [128, 256], "uint16"),
-    "PT0": ("psum", [128, 512], "float32"), "PT1": ("psum", [128, 512], "float32"),
-    "PX0": ("psum", [128, 512], "float32"), "PX1": ("psum", [128, 512], "float32"),
-    "PC": ("psum", [128, 512], "float32"), "PM": ("psum", [128, 512], "float32"), "PN": ("psum", [128, 512], "float32"),
+    "MP": ("sbuf", [128, 32], "float32"),
+    "MR": ("sbuf", [128, 64], "float32"),
+    "PT": ("psum", [128, 512], "float32"),
+    "PX0": ("psum", [128, 512], "float32"), "PX1": ("psum", [128, 512], "float32"), "PX2": ("psum", [128, 512], "float32"),
+    "PC": ("psum", [128, 512], "float32"), "PM0": ("psum", [128, 512], "float32"), "PM1": ("psum", [128, 512], "float32"),
+    "PN": ("psum", [128, 512], "float32"),
 }
-REMOTE = ["ls", "hl", "h0", "h1", "xs", "ps", "l1", "l2", "l3", "b1", "b2", "d0", "d1"]
+REMOTE = ["ls", "h0", "h1", "xs0", "xs1", "ps", "l1", "l2", "l3", "b10", "b11", "b20", "b21", "d0", "d1", "m1", "m2"]
 SEMAPHORES = REMOTE + ["ix", "gp", "go", "ys"] + ["s%d" % i for i in range(100)]
 
 
@@ -78,7 +85,97 @@ def tr(topo, core, src, dst, dests, eng, sem):
         rid, pid = topo.addr(d, core)
         ids.append(DstId(rid=rid, pnc=pid))
     return RemoteDMATransfer(dst_ids=ids, dma_engine_mask=engines(eng), remote_sem=sem, srcs=[src],
-                             dsts=[dst] * len(ids), alu_op=0)
+                             dsts=dst if isinstance(dst, list) else [dst] * len(ids), alu_op=0)
+
+
+def tools(S):
+    used = [0]
+
+    def grp():
+        used[0] += 1
+        return [S["s%d" % (used[0] - 1)], 0]
+
+    def inc(G, inst):
+        inst.then_inc(G[0], 1)
+        G[1] += 1
+
+    def one(inst):
+        G = grp()
+        inc(G, inst)
+        return G
+
+    def wait(queue, *Gs):
+        for G in Gs:
+            queue.wait_ge(G[0], G[1])
+
+    return grp, inc, one, wait
+
+
+def map_constants(g, T, r, tl, width):
+    grp, inc, one, wait = tl
+    v = g.vector
+    gp = one(g.iota(T.PI[:, 0:1], [[0, 1]], 0, 1))
+    gi = grp()
+    inc(gi, g.iota(T.JI[:], [[16, 8]], Z, 0))
+    inc(gi, g.iota(T.MI[:, 0:width], [[1, width]], 0, 0))
+    wait(v, gp)
+    g1 = grp()
+    P = T.PI[:, 0:1]
+    inc(g1, v.tensor_scalar(T.CI[:, 0:1], P, 15, None, A.bitwise_and))
+    inc(g1, v.tensor_scalar(T.CI[:, 1:2], P, 4, None, A.arith_shift_right))
+    inc(g1, v.tensor_scalar(T.CI[:, 2:3], P, 3, 1, A.arith_shift_right, A.bitwise_and))
+    inc(g1, v.tensor_scalar(T.CI[:, 3:4], P, 7, None, A.bitwise_and))
+    inc(g1, v.tensor_scalar(T.CI[:, 4:5], P, 3, None, A.arith_shift_right))
+    inc(g1, v.tensor_scalar(T.CI[:, 5:6], P, 0, None, A.arith_shift_right))
+    wait(v, g1)
+    wait(v, one(v.tensor_copy(T.CF[:, 0:6], T.CI[:, 0:6])))
+    c15, c16, c3, c7, cd8, cp = [T.CF[:, i:i + 1] for i in range(6)]
+    g3 = grp()
+    inc(g3, v.tensor_scalar(T.CG[:, 0:1], c7, 128.0, cd8, A.mult, A.add))
+    inc(g3, v.tensor_scalar(T.CG[:, 1:2], c7, 8.0, c16, A.mult, A.add))
+    wait(v, gi)
+    g4 = grp()
+    inc(g4, v.tensor_scalar(T.IM[:], T.MI[:, 0:128], float(128 * r), None, A.add))
+    inc(g4, v.tensor_copy(T.IN[:], T.MI[:, 0:32]))
+    wait(v, g3)
+    inc(g4, v.tensor_scalar(T.J[:], T.JI[:], T.CG[:, 0:1], None, A.add))
+    return c15, c16, c3, cp, g4
+
+
+def fields(g, T, tl, src, n, o, which):
+    grp, inc, one, wait = tl
+    v = g.vector
+    G = grp()
+    for i, f in enumerate(which):
+        q = T.K[:, o + i * n:o + i * n + n]
+        if f in ("row", "hi"):
+            inc(G, v.tensor_scalar(q, src, 5 if f == "row" else 4, None, A.arith_shift_right))
+        else:
+            inc(G, v.tensor_scalar(q, src, 31 if f == "col" else 15, None, A.bitwise_and))
+    wait(v, G)
+    e = o + len(which) * n
+    return one(v.tensor_copy(T.PL[:, o:e], T.K[:, o:e]))
+
+
+def make_onehot(g, T, tl, i, o):
+    grp, inc, one, wait = tl
+    G = grp()
+    for k in range(8):
+        f = o + k
+        a, b = 1024 * i + 128 * k, 256 * i + 32 * k
+        inc(G, g.vector.tensor_scalar(T.LT[:, a:a + 128], T.IM[:], T.PL[:, f:f + 1], None, A.is_equal))
+        inc(G, g.vector.tensor_scalar(T.RH[:, b:b + 32], T.IN[:], T.PL[:, f + 8:f + 9], T.J[:, k:k + 1], A.is_equal, A.mult))
+    return G
+
+
+def pe_map(g, T, tl, i, onehot):
+    grp, inc, one, wait = tl
+    wait(g.tensor, onehot)
+    G = grp()
+    for k in range(8):
+        a, b = 1024 * i + 128 * k, 256 * i + 32 * k
+        inc(G, g.tensor.matmul(T.PT[:, 0:32], T.LT[:, a:a + 128], T.RH[:, b:b + 32], k == 0, k == 7))
+    return G
 
 
 def rank_program(g, core, T, topo):
@@ -94,29 +191,39 @@ def rank_program(g, core, T, topo):
 
 
 def helper_core(g, core, T, topo, s, mine, way):
-    S = T.sem
+    S, v = T.sem, g.vector
+    tl = grp, inc, one, wait = tools(S)
     _, k, q = peers(topo, T, mine[s])
     far = q if way == 0 else k
     far = sorted(d for d in T.cores if same_chip(topo, d, far))
     off = bits(topo.mask(core, far[0]))
     on = [e for e in bits(topo.mask(core, mine[0])) if e not in off]
-    n = [0]
-    lst = T.HL[:, 0:16]
-    def pl(b): return T.PL[:, 32 * b + 16 * s:32 * b + 16 * s + 16]
-    g.wait_ge(S.hl, len(off) // 2)
-    g.remote_dma_fused([tr(topo, core, lst, pl(1 + way), mine, on, S["l%d" % (1 + way)]),
-                        tr(topo, core, lst, pl(3), [far[s ^ way]], off, S.l3)], local_sem=S.ls)
-    n[0] += len(on) + len(off)
+    b = 1 + way
+    _, _, _, _, g4 = map_constants(g, T, T.rank_of(mine[s]), tl, 128)
+    v.wait_ge(S["l%d" % b], len(off) // 2)
+    wait(v, fields(g, T, tl, T.HL[:, 0:8], 8, 0, ("row", "col")), g4)
+    gm = pe_map(g, T, tl, 0, make_onehot(g, T, tl, 0, 0))
+    t, u = T.PT[:, 0:32], T.U[:]
+    wait(v, gm)
+    wait(v, one(v.tensor_scalar(u, t, 0.0, float(B * b), A.is_gt, A.mult)))
+    gm = one(v.tensor_tensor(T.MP[:], t, u, A.add))
+
+    g.wait_ge(S["l%d" % b], len(off) // 2)
+    g.remote_dma_fused([tr(topo, core, T.HL[:, 4 * s:4 * s + 4], T.IR[:, 16 + 4 * s:20 + 4 * s], [far[s ^ way]], off, S.l3)],
+                       local_sem=S.ls)
+    wait(g, gm)
+    g.remote_dma_fused([tr(topo, core, T.MP[:], T.MR[:, 32 * way:32 * way + 32], [mine[s]], on, S["m%d" % b])], local_sem=S.ls)
+    n = len(off) + len(on)
     for u in ((0, 1) if way == 0 else (1, 0)):
         src = T.H[:, 256 * u:256 * u + 256]
         g.wait_ge(S["h%d" % u], len(off) // 2)
-        t = [tr(topo, core, src, T.V[:, chunk(1 + way, u, s)], mine, on, S["b%d" % (1 + way)])]
-        n[0] += len(on)
+        t = [tr(topo, core, src, T.V[:, chunk(b, u, s)], mine, on, S["b%d%d" % (b, u)])]
+        n += len(on)
         if u == way:
             t = [tr(topo, core, src, T.V[:, chunk(3, u, s)], far, off, S["d%d" % u])] + t
-            n[0] += len(off)
+            n += len(off)
         g.remote_dma_fused(t, local_sem=S.ls)
-    g.wait_ge(S.ls, n[0])
+    g.wait_ge(S.ls, n)
 
 
 def rank_core(g, core, T, topo, s):
@@ -126,19 +233,8 @@ def rank_core(g, core, T, topo, s):
     hr, hc = helpers(topo, rackp)[0], helpers(topo, cablep)[1]
     off = bits(topo.mask(core, hr))
     on = [e for e in bits(topo.mask(core, partner)) if e not in off]
-    used = [0]
-
-    def grp():
-        used[0] += 1
-        return [S["s%d" % (used[0] - 1)], 0]
-
-    def inc(G, inst):
-        inst.then_inc(G[0], 1)
-        G[1] += 1
-
-    def wait(queue, *Gs):
-        for G in Gs:
-            queue.wait_ge(G[0], G[1])
+    even, odd = off[0::2], off[1::2]
+    tl = grp, inc, one, wait = tools(S)
 
     sc.dma_start(T.IX[:], T.idx[:]).then_inc(S.ix, 16)
     for u in range(2):
@@ -148,259 +244,202 @@ def rank_core(g, core, T, topo, s):
         k = 512 * u + 256 * s
         g.sync.dma_start(T.GO[:, 256 * u:256 * u + 256], T.g[:, k:k + 256]).then_inc(S.go, 16)
 
-    gi = grp()
-    inc(gi, g.iota(T.PI[:, 0:1], [[0, 1]], 0, 1))
-    inc(gi, g.iota(T.MI[:], [[1, 128]], 0, 0))
     gz = grp()
     inc(gz, v.memset(T.V[:, 0:Z], 0.0))
-    inc(gz, v.memset(T.TAB[:], 0.0))
-    wait(v, gi)
-    g1 = grp()
-    P = T.PI[:, 0:1]
-    inc(g1, v.tensor_scalar(T.CI[:, 0:1], P, 15, None, A.bitwise_and))
-    inc(g1, v.tensor_scalar(T.CI[:, 1:2], P, 4, None, A.arith_shift_right))
-    inc(g1, v.tensor_scalar(T.CI[:, 2:3], P, 3, 1, A.arith_shift_right, A.bitwise_and))
-    inc(g1, v.tensor_scalar(T.CI[:, 3:4], P, 7, None, A.bitwise_and))
-    inc(g1, v.tensor_scalar(T.CI[:, 4:5], P, 3, None, A.arith_shift_right))
-    inc(g1, v.tensor_scalar(T.CI[:, 5:6], P, 0, None, A.arith_shift_right))
-    inc(g1, v.tensor_scalar(T.IM[:], T.MI[:], float(128 * r), None, A.add))
-    inc(g1, v.tensor_copy(T.IN[:], T.MI[:, 0:32]))
-    wait(v, g1)
-    g2 = grp()
-    inc(g2, v.tensor_copy(T.CF[:, 0:6], T.CI[:, 0:6]))
-    wait(v, g2)
-    c15, c16, c3, c7, cd8, cp = [T.CF[:, i:i + 1] for i in range(6)]
-    g3 = grp()
-    inc(g3, v.tensor_scalar(T.CG[:, 0:1], c7, 128.0, cd8, A.mult, A.add))
-    inc(g3, v.tensor_scalar(T.CG[:, 1:2], c7, 8.0, c16, A.mult, A.add))
-    wait(v, g3)
-    g4 = grp()
-    inc(g4, v.tensor_scalar(T.J0[:], T.MI[:, 0:8], 16.0, T.CG[:, 0:1], A.mult, A.add))
-    wait(v, g4)
-    g5 = grp()
-    inc(g5, v.tensor_scalar(T.J[:], T.J0[:], float(Z), None, A.add))
+    c15, c16, c3, cp, g4 = map_constants(g, T, r, tl, 256)
 
-    gk = grp()
-    v.wait_ge(S.ix, 16)
-    inc(gk, v.tensor_scalar(T.K[:, 0:8], T.IX[:], 5, None, A.arith_shift_right))
-    inc(gk, v.tensor_scalar(T.K[:, 8:16], T.IX[:], 31, None, A.bitwise_and))
-    inc(gk, v.tensor_scalar(T.K[:, 16:24], T.IX[:], 15, None, A.bitwise_and))
-    inc(gk, v.tensor_scalar(T.K[:, 24:32], T.IX[:], 4, None, A.arith_shift_right))
-    wait(v, gk)
-    gl = grp()
-    inc(gl, v.tensor_copy(T.PL[:, 0:32], T.K[:]))
-    wait(v, gl, g5)
+    PX = (T.PX0, T.PX1, T.PX2, T.PX0)
+    PM = (T.PM0, T.PM1)
+    gL, gTR, gX, gTab, gGM, gM, gZ, gN, gPV, gOF, gOU, gE, gC, gEQ = ({} for _ in range(14))
 
-    onehot = {}
-
-    def make_onehot(b):
-        G = onehot[b] = grp()
-        for k in range(8):
-            f = 32 * b + k
-            inc(G, v.tensor_scalar(T.LT[:, 1024 * b + 128 * k:1024 * b + 128 * k + 128], T.IM[:], T.PL[:, f:f + 1], None,
-                                   A.is_equal))
-            inc(G, v.tensor_scalar(T.RH[:, 256 * b + 32 * k:256 * b + 32 * k + 32], T.IN[:], T.PL[:, f + 8:f + 9],
-                                   T.J[:, k:k + 1], A.is_equal, A.mult))
-
-    make_onehot(0)
-    gr = grp()
-    inc(gr, v.tensor_scalar(T.R15[:], T.MI[:], 15, None, A.bitwise_and))
-    inc(gr, v.tensor_scalar(T.R16[:], T.MI[:], 4, None, A.arith_shift_right))
-    inc(gr, v.tensor_scalar(T.R2[:], T.MI[:], 15, 1, A.bitwise_and, A.arith_shift_right))
-    inc(gr, v.tensor_scalar(T.R1[:], T.MI[:], 1, None, A.bitwise_and))
-    inc(gr, v.tensor_scalar(T.R8[:], T.MI[:, 0:16], 8, None, A.bitwise_and))
-    gc = grp()
-    inc(gc, v.tensor_scalar(T.ID[:], T.MI[:], cp, None, A.is_equal))
-    wait(v, gr)
-    inc(gc, v.tensor_scalar(T.RO[:], T.R8[:], 2.0, c15, A.mult, A.add))
-    inc(gc, v.tensor_copy(T.TC[:], T.MI[:, 0:8]))
-    inc(gc, v.tensor_scalar(T.MS[:], T.R15[:], c15, None, A.is_equal))
-    inc(gc, v.tensor_scalar(T.BD[:], T.R16[:], c16, None, A.is_equal))
-    inc(gc, v.tensor_scalar(T.B1[:], T.R2[:], c16, None, A.is_equal))
-    inc(gc, v.tensor_scalar(T.B2[:], T.R1[:], c3, None, A.is_equal))
-    inc(gc, v.tensor_scalar(T.B3[:], T.MI[:, 0:64], T.CG[:, 1:2], None, A.is_equal))
-
-    PT, PX = (T.PT0, T.PT1), (T.PX0, T.PX1)
-    gT, gL, gTR, gX, gTab, gE, gC, gEQ, gGM, gM, gZ, gN, gPV, gOF, gOU, gW = ({} for _ in range(16))
-
-    def pe_map(b):
-        G = gT[b] = grp()
-        wait(te, onehot[b])
-        for k in range(8):
-            inc(G, te.matmul(PT[b % 2][:, 0:32], T.LT[:, 1024 * b + 128 * k:1024 * b + 128 * k + 128],
-                             T.RH[:, 256 * b + 32 * k:256 * b + 32 * k + 32], k == 0, k == 7))
-
-    def merge(b):
-        l = T.L[:, 32 * b:32 * b + 32]
-        t = PT[b % 2][:, 0:32]
-        wait(v, gT[b])
-        if b == 0:
-            G = gL[b] = grp()
-            inc(G, v.tensor_copy(l, t))
-            return
-        u, w = T.U[:, 32 * b:32 * b + 32], T.W[:, 32 * b:32 * b + 32]
-        G = grp()
-        inc(G, v.tensor_scalar(u, t, 0.0, float(B * b), A.is_gt, A.mult))
-        wait(v, G)
-        G = gW[b] = grp()
-        inc(G, v.tensor_tensor(w, t, u, A.add))
-        wait(v, G, gL[b - 1])
-        G = gL[b] = grp()
-        inc(G, v.tensor_tensor(l, w, T.L[:, 32 * b - 32:32 * b], A.max))
+    def last(b):
+        return T.L[:, 32 * b:32 * b + 32]
 
     def spread(b):
         wait(sc, gL[b], gc)
-        G = gTR[b] = grp()
-        inc(G, sc.activation(T.TR[:, 256 * b:256 * b + 256], T.L[:, 32 * b:32 * b + 32].indirect(T.RO[:, 0:16]), AF.Copy))
+        gTR[b] = one(sc.activation(T.TR[:, 256 * b:256 * b + 256], T.L[:, 32 * b:32 * b + 32].indirect(T.RO[:, 0:16]), AF.Copy))
 
     def pe_spread(b):
         G = gX[b] = grp()
         wait(te, gTR[b], gc)
         for h in range(2):
-            inc(G, te.matmul(PX[b % 2][:, 128 * h:128 * h + 128], T.TR[:, 256 * b + 128 * h:256 * b + 128 * h + 128], T.ID[:],
+            inc(G, te.matmul(PX[b][:, 128 * h:128 * h + 128], T.TR[:, 256 * b + 128 * h:256 * b + 128 * h + 128], T.ID[:],
                              True, True))
 
     def table(b):
         G = gTab[b] = grp()
-        wait(v, gX[b], gz)
+        wait(sc, gX[b])
         for h in range(2):
             o = 264 * b + 1 + h
-            inc(G, v.tensor_copy(T.TAB[:, o:o + 255:2], PX[b % 2][:, 128 * h:128 * h + 128]))
+            inc(G, sc.activation(T.TAB[:, o:o + 255:2], PX[b][:, 128 * h:128 * h + 128], AF.Copy))
 
-    def entries(b):
-        q = slice(8 * b, 8 * b + 8)
-        G = gOF[b] = grp()
-        inc(G, v.tensor_scalar(T.OF[:, q], T.PL[:, 32 * b + 24:32 * b + 32], float(256 * r - 1), float(256 * r + 256),
-                               A.max, A.min))
+    def entries(i):
+        n, b = WIDE[i], (0, 1, 3)[i]
+        o = LOHI[i]
+        gOF[i] = one(v.tensor_scalar(T.OF[:, 8 * b:8 * b + n], T.PL[:, o + n:o + 2 * n], float(256 * r - 1),
+                                     float(256 * r + 256), A.max, A.min))
         wait(v, gc)
-        G = gE[b] = grp()
-        inc(G, v.tensor_tensor(T.E[:, 128 * b:128 * b + 128], T.PL[:, 32 * b + 16:32 * b + 24].indirect(T.TC[:, 0:8]), T.MS[:],
-                               A.mult))
-        wait(v, gOF[b])
-        G = gOU[b] = grp()
-        inc(G, v.tensor_scalar(T.OU[:, q], T.OF[:, q], float(1 - 256 * r), None, A.add))
+        gE[i] = one(v.tensor_tensor(T.E[:, 128 * b:128 * b + 16 * n], T.PL[:, o:o + n].indirect(T.TC[:, 0:n]),
+                                    T.MS[:, 0:16 * n], A.mult))
+        wait(v, gOF[i])
+        gOU[i] = one(v.tensor_scalar(T.OU[:, 8 * b:8 * b + n], T.OF[:, 8 * b:8 * b + n], float(1 - 256 * r), None, A.add))
 
-    def pe_entries(b):
-        G = gC[b] = grp()
-        wait(te, gE[b], gc)
-        inc(G, te.matmul(T.PC[:, 0:128], T.BD[:], T.E[:, 128 * b:128 * b + 128], True, True))
+    def pe_entries(i):
+        n, b = 16 * WIDE[i], (0, 1, 3)[i]
+        wait(te, gE[i], gc)
+        gC[i] = one(te.matmul(T.PC[:, 0:n], T.BD[:], T.E[:, 128 * b:128 * b + n], True, True))
+
+    def equal(i):
+        n, b = 16 * WIDE[i], (0, 1, 3)[i]
+        wait(v, gC[i])
+        gEQ[i] = one(v.tensor_scalar(T.EQ[:, 128 * b:128 * b + n], T.PC[:, 0:n], c15, None, A.is_equal))
 
     def lookup(b):
+        i = (0, 1, 1, 2)[b]
+        wait(v, gEQ[i], gTab[b - 1], gOU[i], gz)
         q = slice(128 * b, 128 * b + 128)
-        wait(v, gC[b])
-        G = gEQ[b] = grp()
-        inc(G, v.tensor_scalar(T.EQ[:, q], T.PC[:, 0:128], c15, None, A.is_equal))
-        table(b - 1)
-        wait(v, gEQ[b], gTab[b - 1], gOU[b])
-        G = gGM[b] = grp()
         o = 264 * (b - 1)
-        inc(G, v.tensor_tensor(T.GM[:, q], T.TAB[:, o:o + 258].indirect(T.OU[:, 8 * b:8 * b + 8]), T.EQ[:, q], A.mult))
+        gGM[b] = one(v.tensor_tensor(T.GM[:, q], T.TAB[:, o:o + 258].indirect(T.OU[:, 8 * b:8 * b + 8]), T.EQ[:, q], A.mult))
 
     def pe_pick(b):
-        q = slice(128 * b, 128 * b + 128)
         wait(te, gGM[b])
-        G = gM[b] = grp()
-        inc(G, te.matmul(T.PM[:, 0:128], T.GM[:, q], T.B1[:], True, True))
+        gM[b] = one(te.matmul(PM[b % 2][:, 0:128], T.GM[:, 128 * b:128 * b + 128], T.B1[:], True, True))
 
     def picked(b):
-        q = slice(128 * b, 128 * b + 128)
         wait(v, gM[b])
-        G = gZ[b] = grp()
-        inc(G, v.tensor_tensor(T.ZM[:, q], T.PM[:, 0:128], T.B2[:], A.mult))
+        gZ[b] = one(v.tensor_tensor(T.ZM[:, 128 * b:128 * b + 128], PM[b % 2][:, 0:128], T.B2[:], A.mult))
 
     def pe_place(b):
-        q = slice(128 * b, 128 * b + 128)
         wait(te, gZ[b])
         if b > 1:
             wait(te, gPV[b - 1])
-        G = gN[b] = grp()
-        inc(G, te.matmul(T.PN[:, 0:64], T.ZM[:, q], T.B3[:], True, True))
+        gN[b] = one(te.matmul(T.PN[:, 0:64], T.ZM[:, 128 * b:128 * b + 128], T.B3[:], True, True))
 
     def prev(b):
         wait(v, gN[b])
-        G = gPV[b] = grp()
-        inc(G, v.tensor_copy(T.PV[:, 64 * b:64 * b + 64], T.PN[:, 0:64]))
+        gPV[b] = one(v.tensor_copy(T.PV[:, 64 * b:64 * b + 64], T.PN[:, 0:64]))
 
-    pe_map(0)
-    merge(0)
+    v.wait_ge(S.ix, 16)
+    wait(v, fields(g, T, tl, T.IX[:], 8, BASE[0], ("row", "col")), g4)
+    gT = pe_map(g, T, tl, 0, make_onehot(g, T, tl, 0, BASE[0]))
+    for o in (0, 257):
+        inc(gz, v.tensor_scalar(T.TAB[:, o:o + 529:264], T.MI[:, 0:3], 0.0, None, A.mult))
+    gr = grp()
+    inc(gr, v.tensor_scalar(T.R8[:], T.MI[:, 0:16], 8, None, A.bitwise_and))
+    inc(gr, v.tensor_scalar(T.R15[:], T.MI[:], 15, None, A.bitwise_and))
+    inc(gr, v.tensor_scalar(T.R16[:], T.MI[:, 0:128], 4, None, A.arith_shift_right))
+    inc(gr, v.tensor_scalar(T.R2[:], T.MI[:, 0:128], 15, 1, A.bitwise_and, A.arith_shift_right))
+    inc(gr, v.tensor_scalar(T.R1[:], T.MI[:, 0:128], 1, None, A.bitwise_and))
+    gc = grp()
+    inc(gc, v.tensor_scalar(T.ID[:], T.MI[:, 0:128], cp, None, A.is_equal))
+    inc(gc, v.tensor_copy(T.TC[:], T.MI[:, 0:16]))
+    inc(gc, v.tensor_scalar(T.B3[:], T.MI[:, 0:64], T.CG[:, 1:2], None, A.is_equal))
+    wait(v, gT)
+    gL[0] = one(v.tensor_copy(last(0), T.PT[:, 0:32]))
+    wait(v, gr)
+    inc(gc, v.tensor_scalar(T.RO[:], T.R8[:], 2.0, c15, A.mult, A.add))
+    inc(gc, v.tensor_scalar(T.MS[:], T.R15[:], c15, None, A.is_equal))
+    inc(gc, v.tensor_scalar(T.BD[:], T.R16[:], c16, None, A.is_equal))
+    inc(gc, v.tensor_scalar(T.B1[:], T.R2[:], c16, None, A.is_equal))
+    inc(gc, v.tensor_scalar(T.B2[:], T.R1[:], c3, None, A.is_equal))
     spread(0)
     pe_spread(0)
+    table(0)
 
-    gS = grp()
+    v.wait_ge(S.l1, len(even))
+    v.wait_ge(S.l2, len(odd))
+    wait(v, fields(g, T, tl, T.IR[:, 0:16], 16, BASE[1], ("lo", "hi")))
+    entries(1)
+    pe_entries(1)
+
+    gS = []
     v.wait_ge(S.go, 32)
-    v.wait_ge(S.xs, 16)
     for u in range(2):
         q = slice(256 * u, 256 * u + 256)
-        inc(gS, v.tensor_tensor(T.V[:, chunk(0, u, s)], T.GO[:, q], T.X[:, q], A.add))
+        v.wait_ge(S["xs%d" % u], len(off))
+        gS.append(one(v.tensor_tensor(T.V[:, chunk(0, u, s)], T.GO[:, q], T.X[:, q], A.add)))
 
-    for b in (1, 2, 3):
-        v.wait_ge(S["l%d" % b], 2 * (len(off) if b == 3 else len(on)))
-        make_onehot(b)
-        entries(b)
-        pe_map(b)
-        pe_entries(b)
-        if b > 1:
-            prev(b - 1)
-        lookup(b)
-        pe_pick(b)
-        merge(b)
+    equal(1)
+    lookup(1)
+    pe_pick(1)
+    picked(1)
+    pe_place(1)
+    v.wait_ge(S.l3, 2 * len(off))
+    wait(v, fields(g, T, tl, T.IR[:, 16:24], 8, BASE[2], ("row", "col", "lo", "hi")))
+    entries(2)
+    pe_entries(2)
+    prev(1)
+    for b in (1, 2):
+        v.wait_ge(S["m%d" % b], len(on))
+        wait(v, gL[b - 1])
+        gL[b] = one(v.tensor_tensor(last(b), T.MR[:, 32 * b - 32:32 * b], last(b - 1), A.max))
         spread(b)
         pe_spread(b)
-        picked(b)
-        pe_place(b)
+    table(1)
+    table(2)
+    gT = pe_map(g, T, tl, 1, make_onehot(g, T, tl, 1, BASE[2]))
+    equal(2)
+    lookup(2)
+    pe_pick(2)
+    wait(v, gT)
+    gU = one(v.tensor_scalar(T.U[:], T.PT[:, 0:32], 0.0, float(3 * B), A.is_gt, A.mult))
+    lookup(3)
+    pe_pick(3)
+    picked(2)
+    pe_place(2)
+    wait(v, gU)
+    gW = one(v.tensor_tensor(T.W[:], T.PT[:, 0:32], T.U[:], A.add))
+    picked(3)
+    wait(v, gW, gL[2])
+    gL[3] = one(v.tensor_tensor(last(3), T.W[:], last(2), A.max))
+    spread(3)
+    prev(2)
+    pe_place(3)
+    pe_spread(3)
     prev(3)
-    wait(v, gX[3])
-    gLast = grp()
-    for h in range(2):
-        inc(gLast, v.tensor_copy(T.LST[:, h:h + 255:2], PX[1][:, 128 * h:128 * h + 128]))
-
-    gA = [gS, gz]
 
     def add(b, lo, hi):
-        G = grp()
         k = Z + B * b
-        inc(G, v.tensor_tensor(T.V[:, k + lo:k + hi],
-                               T.V[:, 0:k].indirect(T.PV[:, 64 * b + lo // 16:64 * b + hi // 16]), T.V[:, k + lo:k + hi], A.add))
-        return G
+        return one(v.tensor_tensor(T.V[:, k + lo:k + hi],
+                                   T.V[:, 0:k].indirect(T.PV[:, 64 * b + lo // 16:64 * b + hi // 16]), T.V[:, k + lo:k + hi],
+                                   A.add))
 
-    wait(v, gPV[1], gPV[2], gPV[3], gLast, gS, gz)
+    gLast = grp()
+    wait(v, gPV[1], gS[0], gS[1], gz)
     v.wait_ge(S.ps, 2 * len(on))
-    v.wait_ge(S.b1, 4 * len(on))
-    G = add(1, 0, B)
-    v.wait_ge(S.b2, 4 * len(on))
-    wait(v, G)
-    G = add(2, 0, B)
-    wait(v, G)
-    v.wait_ge(S.d0, 2 * len(off))
-    G0 = add(3, 0, 512)
-    v.wait_ge(S.d1, 2 * len(off))
-    G1 = add(3, 512, B)
+    G = []
+    for b, u in ((1, 0), (1, 1), (2, 1), (2, 0), (3, 0), (3, 1)):
+        if len(G) == 2:
+            if b == 2:
+                wait(v, gX[3])
+                for h in range(2):
+                    inc(gLast, v.tensor_copy(T.LST[:, h:h + 255:2], PX[3][:, 128 * h:128 * h + 128]))
+            wait(v, G[0], G[1], gPV[b])
+            G = []
+        v.wait_ge(S["d%d" % u if b == 3 else "b%d%d" % (b, u)], 2 * len(off if b == 3 else on))
+        G.append(add(b, 512 * u, 512 * u + 512))
 
-    wait(v, G0, G1)
-    wait(sc, G0, G1, gLast)
-    for who, lo, hi in PARTS:
-        G = grp()
-        win = T.V[:].indirect(T.LST[:, lo // 16:hi // 16])
-        if who:
-            inc(G, v.tensor_copy(T.Y[:, lo:hi], win))
-        else:
-            inc(G, sc.activation(T.Y[:, lo:hi], win, AF.Copy))
-        wait(g.sync, G)
-        g.sync.dma_start(T.y[:, lo:hi], T.Y[:, lo:hi]).then_inc(S.ys, 16)
-    g.sync.wait_ge(S.ys, 16 * len(PARTS))
+    wait(v, G[0], G[1], gLast)
+    wait(sc, G[0], G[1], gLast)
+    for lo, hi in zip(CUTS, CUTS[1:]):
+        for who in range(2):
+            a, b = R // 2 * who + lo, R // 2 * who + hi
+            win = T.V[:].indirect(T.LST[:, a // 16:b // 16])
+            H = one(v.tensor_copy(T.Y[:, a:b], win) if who else sc.activation(T.Y[:, a:b], win, AF.Copy))
+            wait(g.sync, H)
+            g.sync.dma_start(T.y[:, a:b], T.Y[:, a:b]).then_inc(S.ys, 16)
+    g.sync.wait_ge(S.ys, 32 * (len(CUTS) - 1))
 
-    wait(g, gl)
-    half = T.PL[:, 16 * s:16 * s + 16]
-    even, odd = off[0::2], off[1::2]
-    g.remote_dma_fused([tr(topo, core, half, T.HL[:, 0:16], [hr], even, S.hl),
-                        tr(topo, core, half, T.HL[:, 0:16], [hc], odd, S.hl)], local_sem=S.ls)
+    g.wait_ge(S.ix, 16)
+    g.remote_dma_fused([tr(topo, core, T.IX[:], [T.IR[:, 0:8], T.HL[:]], [rackp, hr], even, S.l1),
+                        tr(topo, core, T.IX[:], [T.IR[:, 8:16], T.HL[:]], [cablep, hc], odd, S.l2)], local_sem=S.ls)
     n = len(off)
     g.wait_ge(S.gp, 32)
     g.remote_dma_fused([tr(topo, core, T.SEND[:, 256 * u:256 * u + 256], T.X[:, 256 * u:256 * u + 256], [partner],
-                           (off, on)[u], S.xs) for u in range(2)], local_sem=S.ls)
+                           (off, on)[u], S["xs%d" % u]) for u in range(2)], local_sem=S.ls)
     n += len(off) + len(on)
-    wait(g, gS)
     for i in range(2):
+        wait(g, *(gS if i == 0 else gS[1:]))
         a, b = i, 1 - i
         g.remote_dma_fused([
             tr(topo, core, T.V[:, chunk(0, a, s)], T.H[:, 256 * a:256 * a + 256], [hr], even, S["h%d" % a]),

@@ -346,12 +346,6 @@ def rank_core(g, core, T, topo, s):
     pe_spread(0)
     table(0)
 
-    v.wait_ge(S.l1, len(even))
-    v.wait_ge(S.l2, len(odd))
-    wait(v, fields(g, T, tl, T.IR[:, 0:16], 16, BASE[1], ("lo", "hi")))
-    entries(1)
-    pe_entries(1)
-
     gS = []
     v.wait_ge(S.go, 32)
     for u in range(2):
@@ -359,22 +353,27 @@ def rank_core(g, core, T, topo, s):
         v.wait_ge(S["xs%d" % u], len(off))
         gS.append(one(v.tensor_tensor(T.V[:, chunk(0, u, s)], T.GO[:, q], T.X[:, q], A.add)))
 
+    v.wait_ge(S.l1, len(even))
+    v.wait_ge(S.l2, len(odd))
+    wait(v, fields(g, T, tl, T.IR[:, 0:16], 16, BASE[1], ("lo", "hi")))
+    entries(1)
+    pe_entries(1)
     equal(1)
     lookup(1)
     pe_pick(1)
     picked(1)
     pe_place(1)
-    v.wait_ge(S.l3, 2 * len(off))
-    wait(v, fields(g, T, tl, T.IR[:, 16:24], 8, BASE[2], ("row", "col", "lo", "hi")))
-    entries(2)
-    pe_entries(2)
-    prev(1)
     for b in (1, 2):
         v.wait_ge(S["m%d" % b], len(on))
         wait(v, gL[b - 1])
         gL[b] = one(v.tensor_tensor(last(b), T.MR[:, 32 * b - 32:32 * b], last(b - 1), A.max))
         spread(b)
         pe_spread(b)
+    v.wait_ge(S.l3, 2 * len(off))
+    wait(v, fields(g, T, tl, T.IR[:, 16:24], 8, BASE[2], ("row", "col", "lo", "hi")))
+    prev(1)
+    entries(2)
+    pe_entries(2)
     table(1)
     table(2)
     gT = pe_map(g, T, tl, 1, make_onehot(g, T, tl, 1, BASE[2]))
@@ -438,12 +437,18 @@ def rank_core(g, core, T, topo, s):
     g.remote_dma_fused([tr(topo, core, T.SEND[:, 256 * u:256 * u + 256], T.X[:, 256 * u:256 * u + 256], [partner],
                            (off, on)[u], S["xs%d" % u]) for u in range(2)], local_sem=S.ls)
     n += len(off) + len(on)
-    for i in range(2):
-        wait(g, *(gS if i == 0 else gS[1:]))
-        a, b = i, 1 - i
-        g.remote_dma_fused([
-            tr(topo, core, T.V[:, chunk(0, a, s)], T.H[:, 256 * a:256 * a + 256], [hr], even, S["h%d" % a]),
-            tr(topo, core, T.V[:, chunk(0, b, s)], T.H[:, 256 * b:256 * b + 256], [hc], odd, S["h%d" % b]),
-            tr(topo, core, T.V[:, chunk(0, a, s)], T.V[:, chunk(0, a, s)], [partner], on, S.ps)], local_sem=S.ls)
-        n += len(off) + len(on)
+
+    def part(u, way):
+        return tr(topo, core, T.V[:, chunk(0, u, s)], T.H[:, 256 * u:256 * u + 256], [(hr, hc)[way]], (even, odd)[way],
+                  S["h%d" % u])
+
+    def own(u):
+        return tr(topo, core, T.V[:, chunk(0, u, s)], T.V[:, chunk(0, u, s)], [partner], on, S.ps)
+
+    wait(g, gS[0])
+    g.remote_dma_fused([part(0, 0), own(0)], local_sem=S.ls)
+    wait(g, gS[1])
+    g.remote_dma_fused([part(1, 1), own(1)], local_sem=S.ls)
+    g.remote_dma_fused([part(1, 0), part(0, 1)], local_sem=S.ls)
+    n += 2 * len(off) + 2 * len(on)
     g.wait_ge(S.ls, n)

from concourse.bass import DstId, RemoteDMATransfer
from concourse.mybir import AluOpType as A, ActivationFunctionType as AF

B = 1024
Z = 4
VW = Z + 4 * B
R = 4096
CUTS = (0, 320, 1024, 2048)

BASE = (0, 16, 48)
LOHI = (None, 16, 64)
WIDE = (8, 16, 8)

SCRATCH = {
    "V": ("sbuf", [128, VW], "float32"),
    "Y": ("sbuf", [128, R], "float32"),
    "H": ("sbuf", [128, 512], "float32"),
    "SEND": ("sbuf", [128, 512], "float32"),
    "GO": ("sbuf", [128, 512], "float32"),
    "X": ("sbuf", [128, 512], "float32"),
    "IX": ("sbuf", [128, 8], "int32"),
    "IR": ("sbuf", [128, 24], "int32"),
    "HL": ("sbuf", [128, 8], "int32"),
    "K": ("sbuf", [128, 112], "int32"), "PL": ("sbuf", [128, 112], "float32"),
    "PI": ("sbuf", [128, 4], "int32"), "MI": ("sbuf", [128, 256], "int32"), "JI": ("sbuf", [128, 8], "int32"),
    "CI": ("sbuf", [128, 8], "int32"), "CF": ("sbuf", [128, 8], "float32"), "CG": ("sbuf", [128, 4], "float32"),
    "J": ("sbuf", [128, 8], "float32"),
    "IM": ("sbuf", [128, 128], "float16"), "IN": ("sbuf", [128, 32], "float16"),
    "R15": ("sbuf", [128, 256], "int32"), "R16": ("sbuf", [128, 128], "int32"),
    "R2": ("sbuf", [128, 128], "int32"), "R1": ("sbuf", [128, 128], "int32"), "R8": ("sbuf", [128, 16], "int32"),
    "ID": ("sbuf", [128, 128], "float32"), "B1": ("sbuf", [128, 128], "float32"), "B2": ("sbuf", [128, 128], "float32"),
    "B3": ("sbuf", [128, 64], "float32"), "BD": ("sbuf", [128, 128], "bfloat16"), "MS": ("sbuf", [128, 256], "bfloat16"),
    "TC": ("sbuf", [128, 16], "uint16"), "RO": ("sbuf", [128, 16], "uint16"),
    "LT": ("sbuf", [128, 2 * 1024], "float16"), "RH": ("sbuf", [128, 2 * 256], "float16"),
    "L": ("sbuf", [128, 128], "float32"), "U": ("sbuf", [128, 32], "float32"), "W": ("sbuf", [128, 32], "float32"),
    "TR": ("sbuf", [128, 4 * 256], "float32"), "TAB": ("sbuf", [128, 3 * 264], "float32"),
    "OF": ("sbuf", [128, 32], "float32"), "OU": ("sbuf", [128, 32], "uint16"),
    "E": ("sbuf", [128, 512], "bfloat16"), "EQ": ("sbuf", [128, 512], "float32"),
    "GM": ("sbuf", [128, 512], "float32"), "ZM": ("sbuf", [128, 512], "float32"),
    "PV": ("sbuf", [128, 256], "uint16"), "LST": ("sbuf", [128, 256], "uint16"),
    "MP": ("sbuf", [128, 32], "float32"),
    "MR": ("sbuf", [128, 64], "float32"),
    "PT": ("psum", [128, 512], "float32"),
    "PX0": ("psum", [128, 512], "float32"), "PX1": ("psum", [128, 512], "float32"), "PX2": ("psum", [128, 512], "float32"),
    "PC": ("psum", [128, 512], "float32"), "PM0": ("psum", [128, 512], "float32"), "PM1": ("psum", [128, 512], "float32"),
    "PN": ("psum", [128, 512], "float32"),
}
REMOTE = ["ls", "h0", "h1", "xs0", "xs1", "ps", "l1", "l2", "l3", "b10", "b11", "b20", "b21", "d0", "d1", "m1", "m2"]
SEMAPHORES = REMOTE + ["ix", "gp", "go", "ys"] + ["s%d" % i for i in range(100)]


def bits(mask):
    return [i for i in range(16) if mask >> i & 1]


def engines(l):
    return sum(1 << i for i in l)


def same_chip(topo, a, b):
    return topo.host(a) == topo.host(b) and topo.chip(a) == topo.chip(b)


def peers(topo, T, c):
    p = [d for d in T.cores if d != c and same_chip(topo, c, d)][0]
    o = [d for d in T.cores if topo.host(d) != topo.host(c) and topo.die(d) == topo.die(c) and topo.may_write(c, d)]
    k = [d for d in o if topo.rack(topo.host(d)) == topo.rack(topo.host(c))][0]
    q = [d for d in o if topo.rack(topo.host(d)) != topo.rack(topo.host(c))][0]
    return p, k, q


def helpers(topo, c):
    m = [d for d in range(c - 8, c + 9) if d != c and d >= 0 and same_chip(topo, c, d) and topo.die(c) == topo.die(d)]
    return m[-1], m[-2]


def chunk(b, u, s):
    k = Z + B * b + 512 * u + 256 * s
    return slice(k, k + 256)


def tr(topo, core, src, dst, dests, eng, sem):
    ids = []
    for d in dests:
        rid, pid = topo.addr(d, core)
        ids.append(DstId(rid=rid, pnc=pid))
    return RemoteDMATransfer(dst_ids=ids, dma_engine_mask=engines(eng), remote_sem=sem, srcs=[src],
                             dsts=dst if isinstance(dst, list) else [dst] * len(ids), alu_op=0)


def tools(S):
    used = [0]

    def grp():
        used[0] += 1
        return [S["s%d" % (used[0] - 1)], 0]

    def inc(G, inst):
        inst.then_inc(G[0], 1)
        G[1] += 1

    def one(inst):
        G = grp()
        inc(G, inst)
        return G

    def wait(queue, *Gs):
        for G in Gs:
            queue.wait_ge(G[0], G[1])

    return grp, inc, one, wait


def map_constants(g, T, r, tl, width):
    grp, inc, one, wait = tl
    v = g.vector
    gp = one(g.iota(T.PI[:, 0:1], [[0, 1]], 0, 1))
    gi = grp()
    inc(gi, g.iota(T.JI[:], [[16, 8]], Z, 0))
    inc(gi, g.iota(T.MI[:, 0:width], [[1, width]], 0, 0))
    wait(v, gp)
    g1 = grp()
    P = T.PI[:, 0:1]
    inc(g1, v.tensor_scalar(T.CI[:, 0:1], P, 15, None, A.bitwise_and))
    inc(g1, v.tensor_scalar(T.CI[:, 1:2], P, 4, None, A.arith_shift_right))
    inc(g1, v.tensor_scalar(T.CI[:, 2:3], P, 3, 1, A.arith_shift_right, A.bitwise_and))
    inc(g1, v.tensor_scalar(T.CI[:, 3:4], P, 7, None, A.bitwise_and))
    inc(g1, v.tensor_scalar(T.CI[:, 4:5], P, 3, None, A.arith_shift_right))
    inc(g1, v.tensor_scalar(T.CI[:, 5:6], P, 0, None, A.arith_shift_right))
    wait(v, g1)
    wait(v, one(v.tensor_copy(T.CF[:, 0:6], T.CI[:, 0:6])))
    c15, c16, c3, c7, cd8, cp = [T.CF[:, i:i + 1] for i in range(6)]
    g3 = grp()
    inc(g3, v.tensor_scalar(T.CG[:, 0:1], c7, 128.0, cd8, A.mult, A.add))
    inc(g3, v.tensor_scalar(T.CG[:, 1:2], c7, 8.0, c16, A.mult, A.add))
    wait(v, gi)
    g4 = grp()
    inc(g4, v.tensor_scalar(T.IM[:], T.MI[:, 0:128], float(128 * r), None, A.add))
    inc(g4, v.tensor_copy(T.IN[:], T.MI[:, 0:32]))
    wait(v, g3)
    inc(g4, v.tensor_scalar(T.J[:], T.JI[:], T.CG[:, 0:1], None, A.add))
    return c15, c16, c3, cp, g4


def fields(g, T, tl, src, n, o, which):
    grp, inc, one, wait = tl
    v = g.vector
    G = grp()
    for i, f in enumerate(which):
        q = T.K[:, o + i * n:o + i * n + n]
        if f in ("row", "hi"):
            inc(G, v.tensor_scalar(q, src, 5 if f == "row" else 4, None, A.arith_shift_right))
        else:
            inc(G, v.tensor_scalar(q, src, 31 if f == "col" else 15, None, A.bitwise_and))
    wait(v, G)
    e = o + len(which) * n
    return one(v.tensor_copy(T.PL[:, o:e], T.K[:, o:e]))


def make_onehot(g, T, tl, i, o):
    grp, inc, one, wait = tl
    G = grp()
    for k in range(8):
        f = o + k
        a, b = 1024 * i + 128 * k, 256 * i + 32 * k
        inc(G, g.vector.tensor_scalar(T.LT[:, a:a + 128], T.IM[:], T.PL[:, f:f + 1], None, A.is_equal))
        inc(G, g.vector.tensor_scalar(T.RH[:, b:b + 32], T.IN[:], T.PL[:, f + 8:f + 9], T.J[:, k:k + 1], A.is_equal, A.mult))
    return G


def pe_map(g, T, tl, i, onehot):
    grp, inc, one, wait = tl
    wait(g.tensor, onehot)
    G = grp()
    for k in range(8):
        a, b = 1024 * i + 128 * k, 256 * i + 32 * k
        inc(G, g.tensor.matmul(T.PT[:, 0:32], T.LT[:, a:a + 128], T.RH[:, b:b + 32], k == 0, k == 7))
    return G


def rank_program(g, core, T, topo):
    mine = sorted(d for d in T.cores if same_chip(topo, d, core))
    if not mine:
        return
    if T.rank_of(core) is not None:
        return rank_core(g, core, T, topo, mine.index(core))
    for s in range(2):
        hs = helpers(topo, mine[s])
        if core in hs:
            return helper_core(g, core, T, topo, s, mine, hs.index(core))


def helper_core(g, core, T, topo, s, mine, way):
    S, v = T.sem, g.vector
    tl = grp, inc, one, wait = tools(S)
    _, k, q = peers(topo, T, mine[s])
    far = q if way == 0 else k
    far = sorted(d for d in T.cores if same_chip(topo, d, far))
    off = bits(topo.mask(core, far[0]))
    on = [e for e in bits(topo.mask(core, mine[0])) if e not in off]
    b = 1 + way
    _, _, _, _, g4 = map_constants(g, T, T.rank_of(mine[s]), tl, 128)
    v.wait_ge(S["l%d" % b], len(off) // 2)
    wait(v, fields(g, T, tl, T.HL[:, 0:8], 8, 0, ("row", "col")), g4)
    gm = pe_map(g, T, tl, 0, make_onehot(g, T, tl, 0, 0))
    t, u = T.PT[:, 0:32], T.U[:]
    wait(v, gm)
    wait(v, one(v.tensor_scalar(u, t, 0.0, float(B * b), A.is_gt, A.mult)))
    gm = one(v.tensor_tensor(T.MP[:], t, u, A.add))

    g.wait_ge(S["l%d" % b], len(off) // 2)
    g.remote_dma_fused([tr(topo, core, T.HL[:, 4 * s:4 * s + 4], T.IR[:, 16 + 4 * s:20 + 4 * s], [far[s ^ way]], off, S.l3)],
                       local_sem=S.ls)
    wait(g, gm)
    g.remote_dma_fused([tr(topo, core, T.MP[:], T.MR[:, 32 * way:32 * way + 32], [mine[s]], on, S["m%d" % b])], local_sem=S.ls)
    n = len(off) + len(on)
    for u in ((0, 1) if way == 0 else (1, 0)):
        src = T.H[:, 256 * u:256 * u + 256]
        g.wait_ge(S["h%d" % u], len(off) // 2)
        t = [tr(topo, core, src, T.V[:, chunk(b, u, s)], mine, on, S["b%d%d" % (b, u)])]
        n += len(on)
        if u == way:
            t = [tr(topo, core, src, T.V[:, chunk(3, u, s)], far, off, S["d%d" % u])] + t
            n += len(off)
        g.remote_dma_fused(t, local_sem=S.ls)
    g.wait_ge(S.ls, n)


def rank_core(g, core, T, topo, s):
    S, v, te, sc = T.sem, g.vector, g.tensor, g.scalar
    r = T.rank_of(core)
    partner, rackp, cablep = peers(topo, T, core)
    hr, hc = helpers(topo, rackp)[0], helpers(topo, cablep)[1]
    off = bits(topo.mask(core, hr))
    on = [e for e in bits(topo.mask(core, partner)) if e not in off]
    even, odd = off[0::2], off[1::2]
    tl = grp, inc, one, wait = tools(S)

    sc.dma_start(T.IX[:], T.idx[:]).then_inc(S.ix, 16)
    for u in range(2):
        k = 512 * u + 256 * (1 - s)
        g.sync.dma_start(T.SEND[:, 256 * u:256 * u + 256], T.g[:, k:k + 256]).then_inc(S.gp, 16)
    for u in range(2):
        k = 512 * u + 256 * s
        g.sync.dma_start(T.GO[:, 256 * u:256 * u + 256], T.g[:, k:k + 256]).then_inc(S.go, 16)

    gz = grp()
    inc(gz, v.memset(T.V[:, 0:Z], 0.0))
    c15, c16, c3, cp, g4 = map_constants(g, T, r, tl, 256)

    PX = (T.PX0, T.PX1, T.PX2, T.PX0)
    PM = (T.PM0, T.PM1)
    gL, gTR, gX, gTab, gGM, gM, gZ, gN, gPV, gOF, gOU, gE, gC, gEQ = ({} for _ in range(14))

    def last(b):
        return T.L[:, 32 * b:32 * b + 32]

    def spread(b):
        wait(sc, gL[b], gc)
        gTR[b] = one(sc.activation(T.TR[:, 256 * b:256 * b + 256], T.L[:, 32 * b:32 * b + 32].indirect(T.RO[:, 0:16]), AF.Copy))

    def pe_spread(b):
        G = gX[b] = grp()
        wait(te, gTR[b], gc)
        for h in range(2):
            inc(G, te.matmul(PX[b][:, 128 * h:128 * h + 128], T.TR[:, 256 * b + 128 * h:256 * b + 128 * h + 128], T.ID[:],
                             True, True))

    def table(b):
        G = gTab[b] = grp()
        wait(sc, gX[b])
        for h in range(2):
            o = 264 * b + 1 + h
            inc(G, sc.activation(T.TAB[:, o:o + 255:2], PX[b][:, 128 * h:128 * h + 128], AF.Copy))

    def entries(i):
        n, b = WIDE[i], (0, 1, 3)[i]
        o = LOHI[i]
        gOF[i] = one(v.tensor_scalar(T.OF[:, 8 * b:8 * b + n], T.PL[:, o + n:o + 2 * n], float(256 * r - 1),
                                     float(256 * r + 256), A.max, A.min))
        wait(v, gc)
        gE[i] = one(v.tensor_tensor(T.E[:, 128 * b:128 * b + 16 * n], T.PL[:, o:o + n].indirect(T.TC[:, 0:n]),
                                    T.MS[:, 0:16 * n], A.mult))
        wait(v, gOF[i])
        gOU[i] = one(v.tensor_scalar(T.OU[:, 8 * b:8 * b + n], T.OF[:, 8 * b:8 * b + n], float(1 - 256 * r), None, A.add))

    def pe_entries(i):
        n, b = 16 * WIDE[i], (0, 1, 3)[i]
        wait(te, gE[i], gc)
        gC[i] = one(te.matmul(T.PC[:, 0:n], T.BD[:], T.E[:, 128 * b:128 * b + n], True, True))

    def equal(i):
        n, b = 16 * WIDE[i], (0, 1, 3)[i]
        wait(v, gC[i])
        gEQ[i] = one(v.tensor_scalar(T.EQ[:, 128 * b:128 * b + n], T.PC[:, 0:n], c15, None, A.is_equal))

    def lookup(b):
        i = (0, 1, 1, 2)[b]
        wait(v, gEQ[i], gTab[b - 1], gOU[i], gz)
        q = slice(128 * b, 128 * b + 128)
        o = 264 * (b - 1)
        gGM[b] = one(v.tensor_tensor(T.GM[:, q], T.TAB[:, o:o + 258].indirect(T.OU[:, 8 * b:8 * b + 8]), T.EQ[:, q], A.mult))

    def pe_pick(b):
        wait(te, gGM[b])
        gM[b] = one(te.matmul(PM[b % 2][:, 0:128], T.GM[:, 128 * b:128 * b + 128], T.B1[:], True, True))

    def picked(b):
        wait(v, gM[b])
        gZ[b] = one(v.tensor_tensor(T.ZM[:, 128 * b:128 * b + 128], PM[b % 2][:, 0:128], T.B2[:], A.mult))

    def pe_place(b):
        wait(te, gZ[b])
        if b > 1:
            wait(te, gPV[b - 1])
        gN[b] = one(te.matmul(T.PN[:, 0:64], T.ZM[:, 128 * b:128 * b + 128], T.B3[:], True, True))

    def prev(b):
        wait(v, gN[b])
        gPV[b] = one(v.tensor_copy(T.PV[:, 64 * b:64 * b + 64], T.PN[:, 0:64]))

    v.wait_ge(S.ix, 16)
    wait(v, fields(g, T, tl, T.IX[:], 8, BASE[0], ("row", "col")), g4)
    gT = pe_map(g, T, tl, 0, make_onehot(g, T, tl, 0, BASE[0]))
    for o in (0, 257):
        inc(gz, v.tensor_scalar(T.TAB[:, o:o + 529:264], T.MI[:, 0:3], 0.0, None, A.mult))
    gr = grp()
    inc(gr, v.tensor_scalar(T.R8[:], T.MI[:, 0:16], 8, None, A.bitwise_and))
    inc(gr, v.tensor_scalar(T.R15[:], T.MI[:], 15, None, A.bitwise_and))
    inc(gr, v.tensor_scalar(T.R16[:], T.MI[:, 0:128], 4, None, A.arith_shift_right))
    inc(gr, v.tensor_scalar(T.R2[:], T.MI[:, 0:128], 15, 1, A.bitwise_and, A.arith_shift_right))
    inc(gr, v.tensor_scalar(T.R1[:], T.MI[:, 0:128], 1, None, A.bitwise_and))
    gc = grp()
    inc(gc, v.tensor_scalar(T.ID[:], T.MI[:, 0:128], cp, None, A.is_equal))
    inc(gc, v.tensor_copy(T.TC[:], T.MI[:, 0:16]))
    inc(gc, v.tensor_scalar(T.B3[:], T.MI[:, 0:64], T.CG[:, 1:2], None, A.is_equal))
    wait(v, gT)
    gL[0] = one(v.tensor_copy(last(0), T.PT[:, 0:32]))
    wait(v, gr)
    inc(gc, v.tensor_scalar(T.RO[:], T.R8[:], 2.0, c15, A.mult, A.add))
    inc(gc, v.tensor_scalar(T.MS[:], T.R15[:], c15, None, A.is_equal))
    inc(gc, v.tensor_scalar(T.BD[:], T.R16[:], c16, None, A.is_equal))
    inc(gc, v.tensor_scalar(T.B1[:], T.R2[:], c16, None, A.is_equal))
    inc(gc, v.tensor_scalar(T.B2[:], T.R1[:], c3, None, A.is_equal))
    spread(0)
    pe_spread(0)
    table(0)

    gS = []
    v.wait_ge(S.go, 32)
    for u in range(2):
        q = slice(256 * u, 256 * u + 256)
        v.wait_ge(S["xs%d" % u], len(off))
        gS.append(one(v.tensor_tensor(T.V[:, chunk(0, u, s)], T.GO[:, q], T.X[:, q], A.add)))

    v.wait_ge(S.l1, len(even))
    v.wait_ge(S.l2, len(odd))
    wait(v, fields(g, T, tl, T.IR[:, 0:16], 16, BASE[1], ("lo", "hi")))
    entries(1)
    pe_entries(1)
    equal(1)
    lookup(1)
    pe_pick(1)
    picked(1)
    pe_place(1)
    for b in (1, 2):
        v.wait_ge(S["m%d" % b], len(on))
        wait(v, gL[b - 1])
        gL[b] = one(v.tensor_tensor(last(b), T.MR[:, 32 * b - 32:32 * b], last(b - 1), A.max))
        spread(b)
        pe_spread(b)
    v.wait_ge(S.l3, 2 * len(off))
    wait(v, fields(g, T, tl, T.IR[:, 16:24], 8, BASE[2], ("row", "col", "lo", "hi")))
    prev(1)
    entries(2)
    pe_entries(2)
    table(1)
    table(2)
    gT = pe_map(g, T, tl, 1, make_onehot(g, T, tl, 1, BASE[2]))
    equal(2)
    lookup(2)
    pe_pick(2)
    wait(v, gT)
    gU = one(v.tensor_scalar(T.U[:], T.PT[:, 0:32], 0.0, float(3 * B), A.is_gt, A.mult))
    lookup(3)
    pe_pick(3)
    picked(2)
    pe_place(2)
    wait(v, gU)
    gW = one(v.tensor_tensor(T.W[:], T.PT[:, 0:32], T.U[:], A.add))
    picked(3)
    wait(v, gW, gL[2])
    gL[3] = one(v.tensor_tensor(last(3), T.W[:], last(2), A.max))
    spread(3)
    prev(2)
    pe_place(3)
    pe_spread(3)
    prev(3)

    def add(b, lo, hi):
        k = Z + B * b
        return one(v.tensor_tensor(T.V[:, k + lo:k + hi],
                                   T.V[:, 0:k].indirect(T.PV[:, 64 * b + lo // 16:64 * b + hi // 16]), T.V[:, k + lo:k + hi],
                                   A.add))

    gLast = grp()
    wait(v, gPV[1], gS[0], gS[1], gz)
    v.wait_ge(S.ps, 2 * len(on))
    G = []
    for b, u in ((1, 0), (1, 1), (2, 1), (2, 0), (3, 0), (3, 1)):
        if len(G) == 2:
            if b == 2:
                wait(v, gX[3])
                for h in range(2):
                    inc(gLast, v.tensor_copy(T.LST[:, h:h + 255:2], PX[3][:, 128 * h:128 * h + 128]))
            wait(v, G[0], G[1], gPV[b])
            G = []
        v.wait_ge(S["d%d" % u if b == 3 else "b%d%d" % (b, u)], 2 * len(off if b == 3 else on))
        G.append(add(b, 512 * u, 512 * u + 512))

    wait(v, G[0], G[1], gLast)
    wait(sc, G[0], G[1], gLast)
    for lo, hi in zip(CUTS, CUTS[1:]):
        for who in range(2):
            a, b = R // 2 * who + lo, R // 2 * who + hi
            win = T.V[:].indirect(T.LST[:, a // 16:b // 16])
            H = one(v.tensor_copy(T.Y[:, a:b], win) if who else sc.activation(T.Y[:, a:b], win, AF.Copy))
            wait(g.sync, H)
            g.sync.dma_start(T.y[:, a:b], T.Y[:, a:b]).then_inc(S.ys, 16)
    g.sync.wait_ge(S.ys, 32 * (len(CUTS) - 1))

    g.wait_ge(S.ix, 16)
    g.remote_dma_fused([tr(topo, core, T.IX[:], [T.IR[:, 0:8], T.HL[:]], [rackp, hr], even, S.l1),
                        tr(topo, core, T.IX[:], [T.IR[:, 8:16], T.HL[:]], [cablep, hc], odd, S.l2)], local_sem=S.ls)
    n = len(off)
    g.wait_ge(S.gp, 32)
    g.remote_dma_fused([tr(topo, core, T.SEND[:, 256 * u:256 * u + 256], T.X[:, 256 * u:256 * u + 256], [partner],
                           (off, on)[u], S["xs%d" % u]) for u in range(2)], local_sem=S.ls)
    n += len(off) + len(on)

    def part(u, way):
        return tr(topo, core, T.V[:, chunk(0, u, s)], T.H[:, 256 * u:256 * u + 256], [(hr, hc)[way]], (even, odd)[way],
                  S["h%d" % u])

    def own(u):
        return tr(topo, core, T.V[:, chunk(0, u, s)], T.V[:, chunk(0, u, s)], [partner], on, S.ps)

    wait(g, gS[0])
    g.remote_dma_fused([part(0, 0), own(0)], local_sem=S.ls)
    wait(g, gS[1])
    g.remote_dma_fused([part(1, 1), own(1)], local_sem=S.ls)
    g.remote_dma_fused([part(1, 0), part(0, 1)], local_sem=S.ls)
    n += 2 * len(off) + 2 * len(on)
    g.wait_ge(S.ls, n)
